import numpy as np
import ml_dtypes


def mxq(x, axis, fmt="e4m3"):
    dtype, down = {"e4m3": (ml_dtypes.float8_e4m3fn, 7), "e5m2": (ml_dtypes.float8_e5m2, 14)}[fmt]
    v = np.moveaxis(np.asarray(x, np.float32).astype(ml_dtypes.bfloat16).astype(np.float64), axis, -1)
    blocks = v.reshape(v.shape[:-1] + (-1, 32))
    amax = np.abs(blocks).max(-1, keepdims=True)
    byte = np.maximum(np.where(amax > 0, np.frexp(amax)[1] - 1 + 127, 0) - down, 1)
    scale = np.exp2(byte - 127.0)
    codes = (blocks / scale).astype(np.float32).astype(dtype).astype(np.float64)
    return np.moveaxis((codes * scale).reshape(v.shape), -1, axis)


WIDE = False


def mx_kscale(k):
    if not WIDE:
        return np.ones(k)
    levels = np.array([10, -10, 5, -5, 0])
    if k % 512:
        return np.exp2(np.random.permutation(np.resize(levels, k // 32))).repeat(32)
    a = np.empty((k // 512, 16))
    for p in range(k // 512):
        a[p, :8] = np.random.permutation(np.resize(levels, 8))
        for g in range(8):
            far = levels[np.abs(levels - a[p, g]) >= 10]
            a[p, g + 8] = far[np.random.randint(len(far))]
    return np.exp2(a.ravel()).repeat(32)


def f64(x):
    return np.asarray(x).astype(np.float64)


def striped(idx):
    return np.tile(np.asarray(idx).reshape(-1, 16).T, (8, 1)).astype(np.uint16)


def unstriped(offs):
    return offs[:16].T.reshape(-1).astype(np.int64)


def striped8(idx):
    return np.asarray(idx).reshape(8, -1, 16).transpose(0, 2, 1).reshape(128, -1).astype(np.uint16)


def unstriped8(offs):
    return offs.reshape(8, 16, -1).transpose(0, 2, 1).reshape(8, -1).astype(np.int64)


def pick8(x, idx, run):
    r = np.arange(len(x))
    return x[r[:, None], idx[r % (8 * run) // run]]


E2M1 = np.array([0.0, 0.5, 1.0, 1.5, 2.0, 3.0, 4.0, 6.0, -0.0, -0.5, -1.0, -1.5, -2.0, -3.0, -4.0, -6.0])


def pack_weight(w, fmt):
    k, n = w.shape
    w = f64(np.asarray(w, np.float32).astype(ml_dtypes.bfloat16)).reshape(k // 32, 32, n)
    amax = np.abs(w).max(1)
    if fmt == "e4m3":
        byte = np.frexp(amax)[1] - 1 + 127 - 7
    else:
        mant, ex = np.frexp(amax / 6.0)
        byte = np.where(mant > 0.5, ex, ex - 1) + 127
    byte = np.clip(np.where(amax > 0, byte, 1), 1, 254)
    scaled = (w * np.exp2(127.0 - byte)[:, None, :]).reshape(k, n).astype(np.float32)
    by_word = np.ascontiguousarray(scaled.reshape(k // 512, 128, 4, n).transpose(0, 1, 3, 2))
    if fmt == "e4m3":
        words = by_word.astype(ml_dtypes.float8_e4m3fn).view(np.uint8)
    else:
        c = by_word.astype(ml_dtypes.float4_e2m1fn).view(np.uint8) & 0xF
        words = (c[..., 0::2] | (c[..., 1::2] << 4)).reshape(k // 512, 128, 2 * n)
    return np.ascontiguousarray(words), np.ascontiguousarray(byte.astype(np.uint8).reshape(k // 512, 16, n))


def unpack_weight(words, scales, fmt):
    g, _, n = scales.shape
    words = np.ascontiguousarray(words).reshape(g, 128, n, -1)
    if fmt == "e4m3":
        vals = words.view(ml_dtypes.float8_e4m3fn).astype(np.float64)
    else:
        nib = np.empty((g, 128, n, 4), np.uint8)
        nib[..., 0::2] = words & 0xF
        nib[..., 1::2] = words >> 4
        vals = E2M1[nib]
    vals = vals * np.repeat(np.exp2(scales.astype(np.float64) - 127.0), 8, axis=1)[..., None]
    return vals.transpose(0, 1, 3, 2).reshape(g * 512, n)


def sigmoid(v):
    return 1.0 / (1.0 + np.exp(-v))


K, R, F, T, J, M, G = 512, 128, 512, 2048, 512, 256, 32


def setup_inputs():
    n = np.random.standard_normal
    idx = np.random.permutation(T)[:J]
    idx2 = np.stack([np.random.permutation(J)[:M] for _ in range(8)])
    fk = mx_kscale(K)
    ff = mx_kscale(F)
    tabp = pack_weight(n((K, T)) / fk[:, None], "e2m1")
    return {
        "tab_words": tabp[0],
        "tab_scales": tabp[1],
        "w1": (n((K, R)) * 1 / np.sqrt(K) * fk[:, None]).astype(np.float32),
        "gain": (np.random.uniform(0.5, 1.5, (R, 1))).astype(np.float32),
        "share": (np.random.uniform(0.4, 1.0, (R, 1))).astype(np.float32),
        "pb": (np.random.uniform(-0.5, 0.5, (1, M))).astype(np.float32),
        "wo": (n((F, R)) * 1 / np.sqrt(F) * ff[:, None]).astype(np.float32),
        "dy": (n((F, M)) / ff[:, None]).astype(np.float32),
        "old": (0.5 * n((R, J))).astype(np.float32),
        "offs": striped(idx),
        "offs2": striped8(idx2),
    }


def reference(tab_words, tab_scales, w1, gain, share, pb, wo, dy, old, offs, offs2):
    idx = unstriped(offs)
    idx2 = unstriped8(offs2)
    tabu = unpack_weight(tab_words, tab_scales, "e2m1")
    w1q = mxq(f64(w1), 0, "e4m3")
    tabidxg = tabu[:, idx]
    a = w1q.T @ tabidxg
    h0 = np.tanh(a)
    h1 = h0 * f64(gain)
    s = pick8(h1, idx2, 16) + f64(pb)
    m1 = s.reshape(R, G, M // G).mean(axis=2)
    mr = np.repeat(m1, M // G, axis=1)
    woq = mxq(f64(wo), 0, "e4m3")
    dyq = mxq(f64(dy), 0, "e4m3")
    c0 = woq.T @ dyq
    dmr = c0 * sigmoid(s - mr * f64(share)) * (-1.0) * f64(share)
    dm1 = dmr.reshape(R, G, M // G).sum(axis=2)
    e1 = dm1 / 8.0
    r1 = np.repeat(e1, M // G, axis=1)
    ds = c0 * sigmoid(s - mr * f64(share)) + r1
    s2 = np.zeros((R, J))
    s2[np.arange(R)[:, None], idx2[np.arange(R) % 128 // 16]] = ds
    dh0 = s2 * f64(gain)
    da = dh0 * (1.0 - np.square(h0))
    y = da + f64(old)
    return y

@@ -1,0 +1,182 @@
+import math
+from contextlib import ExitStack
+
+import concourse.mybir as mybir
+from concourse.masks import make_identity
+
+K, R, F, T, J, M, G = 512, 128, 512, 2048, 512, 256, 32
+FLOPS = 2 * K * R * J + 2 * F * R * M
+
+F32 = mybir.dt.float32
+BF16 = mybir.dt.bfloat16
+I32 = mybir.dt.int32
+U32 = mybir.dt.uint32
+U16 = mybir.dt.uint16
+U8 = mybir.dt.uint8
+FP8X4 = mybir.dt.float8_e4m3fn_x4
+FP4X4 = mybir.dt.float4_e2m1fn_x4
+ALU = mybir.AluOpType
+ACT = mybir.ActivationFunctionType
+
+P = 128
+PACK = 4
+RUN = M // G
+LIST = 16
+
+
+def woven(grouped, raw):
+    return (
+        grouped.rearrange("p (c i) t -> p c t i", i=4),
+        raw.rearrange("p t (c i) -> p c t i", i=4),
+    )
+
+
+def tile_attend_cpickcentred_kernel(tc, tab_words, tab_scales, w1, gain, share, pb, wo, dy, old, offs, offs2, out):
+    nc = tc.nc
+    JH = J // 2
+    MH = M // 2
+    GH = G // 2
+    with ExitStack() as ctx:
+        sb = ctx.enter_context(tc.tile_pool(name="sb", bufs=1))
+        late = ctx.enter_context(tc.tile_pool(name="late", bufs=1))
+        ps = ctx.enter_context(tc.psum_pool(name="ps", bufs=1))
+
+        idx = sb.tile([P, J // LIST], U16, name="idx")
+        idx2 = sb.tile([P, M // LIST], U16, name="idx2")
+        words = late.tile([P, T], U16, name="words", align_bytes=64, offset=0)
+        scales = sb.tile([P, T], U8, name="scales", align_bytes=64)
+        placed = sb.tile([P, J], F32, name="placed")
+        dy_raw = sb.tile([P, PACK, M], F32, name="dy_raw")
+        w1_raw = sb.tile([P, PACK, R], F32, name="w1_raw", tag="w1_then_old")
+        pb_cols = sb.tile([P, 2], F32, name="pb_cols")
+        ident = sb.tile([P, P], F32, name="ident")
+
+        nc.vector.memset(scales[:].bitcast(I32), 0)
+        nc.vector.memset(placed[:], 0.0)
+        share_sb = sb.tile([P, 1], F32, name="share_sb")
+        centre = sb.tile([P, 1], F32, name="centre")
+        nc.gpsimd.dma_start(share_sb[:], share)
+        nc.gpsimd.dma_start(pb_cols[:], pb.rearrange("o (p e) -> p (o e)", e=2))
+        make_identity(nc, ident[:])
+        nc.gpsimd.tensor_scalar(centre[:], share_sb[:], -1.0 / RUN, 0.0, ALU.mult, ALU.add)
+        nc.sync.dma_start(idx[:], offs)
+        nc.sync.dma_start(words[:].bitcast(I32), tab_words[0].bitcast(I32))
+        nc.sync.dma_start(w1_raw[:], w1.rearrange("(p t) r -> p t r", t=PACK))
+        nc.sync.dma_start(idx2[:], offs2)
+        nc.sync.dma_start(dy_raw[:], dy.rearrange("(p t) m -> p t m", t=PACK))
+        for q in range(4):
+            nc.scalar.dma_start(
+                scales[32 * q : 32 * q + 4, :].bitcast(I32), tab_scales[0, 4 * q : 4 * q + 4, :].bitcast(I32)
+            )
+
+        def operand(name, width, pool=sb, offset=None):
+            grouped = pool.tile([P, width, PACK], BF16, name=name + "_bf", align_bytes=64, offset=offset)
+            codes = sb.tile([P, width], U32, name=name + "_codes", align_bytes=64)
+            plane = sb.tile([P, width], U8, name=name + "_plane", align_bytes=64)
+            return grouped, codes, plane
+
+        def quantise(op):
+            grouped, codes, plane = op
+            nc.vector.quantize_mx(codes[:].bitcast(FP8X4), plane[:], grouped[:].rearrange("p c t -> p (c t)"))
+
+        w1_q = operand("w1", R)
+        dy_q = operand("dy", M, late, 5120)
+
+        got_words = late.tile([P, J], U16, name="got_words", align_bytes=64, offset=4096)
+        got_scales = [sb.tile([P, JH], U8, name="got_scales%d" % h, align_bytes=64) for h in range(2)]
+        a_ps = [ps.tile([P, JH], F32, name="a_ps%d" % h) for h in range(2)]
+        c_ps = ps.tile([P, M], F32, name="c_ps")
+        pb_ps = ps.tile([P, 2, P], F32, name="pb_ps")
+        h0 = sb.tile([P, J], F32, name="h0")
+        h0_sq = sb.tile([P, J], F32, name="h0_sq")
+        pb_rows = sb.tile([P, M], F32, name="pb_rows")
+
+        dst, src = woven(w1_q[0][:], w1_raw[:])
+        nc.scalar.activation(dst, src, ACT.Copy)
+        nc.vector.tensor_copy(got_words[:], words[:].indirect(idx[:]))
+        gain_sb = late.tile([P, 1], F32, name="gain_sb", offset=0)
+        wo_raw = late.tile([P, PACK, R], F32, name="wo_raw", offset=128)
+        nc.sync.dma_start(gain_sb[:], gain)
+        nc.sync.dma_start(wo_raw[:], wo.rearrange("(p t) r -> p t r", t=PACK))
+        old_sb = sb.tile([P, J], F32, name="old_sb", tag="w1_then_old")
+        nc.sync.dma_start(old_sb[:], old)
+        quantise(w1_q)
+        for h in range(2):
+            nc.vector.tensor_copy(got_scales[h][:], scales[:].indirect(idx[:, h * JH // LIST : (h + 1) * JH // LIST]))
+
+        for h in range(2):
+            cols = slice(h * JH, (h + 1) * JH)
+            nc.tensor.matmul_mx(
+                a_ps[h][:],
+                lhsT=w1_q[1][:].bitcast(FP8X4),
+                lhsT_scale=w1_q[2][:],
+                rhs=got_words[:, cols].bitcast(FP4X4),
+                rhs_scale=got_scales[h][:],
+                start=True,
+                stop=True,
+            )
+            nc.scalar.activation(h0[:, cols], a_ps[h][:], ACT.Tanh)
+
+        for e in range(2):
+            nc.tensor.transpose(pb_ps[:, e, :], pb_cols[:, e : e + 1].to_broadcast([P, P]), ident[:])
+        nc.scalar.copy(pb_rows[:].rearrange("r (p e) -> r p e", e=2), pb_ps[:].rearrange("r e p -> r p e"))
+
+        dst, src = woven(dy_q[0][:], dy_raw[:])
+        nc.vector.tensor_copy(dst, src)
+        quantise(dy_q)
+        h1 = late.tile([P, J], F32, name="h1", offset=5120)
+        for h in range(2):
+            cols = slice(h * JH, (h + 1) * JH)
+            nc.vector.tensor_scalar(h1[:, cols], h0[:, cols], gain_sb[:], None, ALU.mult)
+        wo_q = operand("wo", R, late, 4096)
+        dst, src = woven(wo_q[0][:], wo_raw[:])
+        nc.scalar.activation(dst, src, ACT.Copy)
+        quantise(wo_q)
+        nc.tensor.matmul_mx(
+            c_ps[:],
+            lhsT=wo_q[1][:].bitcast(FP8X4),
+            lhsT_scale=wo_q[2][:],
+            rhs=dy_q[1][:].bitcast(FP8X4),
+            rhs_scale=dy_q[2][:],
+            start=True,
+            stop=True,
+        )
+
+        def halves(name, width):
+            return [sb.tile([P, width], F32, name="%s%d" % (name, h)) for h in range(2)]
+
+        s, z, th, g2, r2 = (halves(n, MH) for n in ("s", "z", "th", "g2", "r2"))
+        s_sum, g_sum = halves("s_sum", GH), halves("g_sum", GH)
+        picks = [idx2[:, h * MH // LIST : (h + 1) * MH // LIST] for h in range(2)]
+
+        def runs(tile):
+            return tile[:].rearrange("r (g e) -> r g e", e=RUN)
+
+        def spread(tile):
+            return tile[:].unsqueeze(2).to_broadcast([P, GH, RUN])
+
+        for h in range(2):
+            nc.vector.tensor_tensor(s[h][:], h1[:].indirect(picks[h]), pb_rows[:, h * MH : (h + 1) * MH], ALU.add)
+        for h in range(2):
+            nc.vector.tensor_reduce(s_sum[h][:], runs(s[h]), mybir.AxisListType.X, ALU.add)
+        for h in range(2):
+            nc.vector.scalar_tensor_tensor(runs(z[h]), spread(s_sum[h]), centre[:], runs(s[h]), ALU.mult, ALU.add)
+            nc.scalar.activation(th[h][:], z[h][:], ACT.Tanh, scale=-0.5)
+        nc.scalar.activation(h0_sq[:], h0[:], ACT.Square, scale=math.sqrt(0.5))
+        for h in range(2):
+            nc.vector.scalar_tensor_tensor(g2[h][:], th[h][:], 1.0, c_ps[:, h * MH : (h + 1) * MH], ALU.subtract, ALU.mult)
+        for h in range(2):
+            nc.vector.tensor_reduce(g_sum[h][:], runs(g2[h]), mybir.AxisListType.X, ALU.add)
+        for h in range(2):
+            nc.vector.tensor_scalar(runs(r2[h]), spread(g_sum[h]), centre[:], None, ALU.mult)
+        for h in range(2):
+            nc.vector.tensor_tensor(placed[:].indirect(picks[h]), g2[h][:], r2[h][:], ALU.add)
+
+        da, res = halves("da", JH), halves("res", JH)
+        for h in range(2):
+            cols = slice(h * JH, (h + 1) * JH)
+            nc.vector.scalar_tensor_tensor(da[h][:], h0_sq[:, cols], 0.5, placed[:, cols], ALU.subtract, ALU.mult)
+        for h, queue in enumerate((nc.sync, nc.scalar)):
+            cols = slice(h * JH, (h + 1) * JH)
+            nc.vector.scalar_tensor_tensor(res[h][:], da[h][:], gain_sb[:], old_sb[:, cols], ALU.mult, ALU.add)
+            queue.dma_start(out[:, cols], res[h][:])

@@ -2,7 +2,6 @@ import math
 from contextlib import ExitStack
 
 import concourse.mybir as mybir
-from concourse.masks import make_identity
 
 K, R, F, T, J, M, G = 512, 128, 512, 2048, 512, 256, 32
 FLOPS = 2 * K * R * J + 2 * F * R * M
@@ -43,73 +42,80 @@ def tile_attend_cpickcentred_kernel(tc, tab_words, tab_scales, w1, gain, share, 
 
         idx = sb.tile([P, J // LIST], U16, name="idx")
         idx2 = sb.tile([P, M // LIST], U16, name="idx2")
-        words = late.tile([P, T], U16, name="words", align_bytes=64, offset=0)
-        scales = sb.tile([P, T], U8, name="scales", align_bytes=64)
-        placed = sb.tile([P, J], F32, name="placed")
-        dy_raw = sb.tile([P, PACK, M], F32, name="dy_raw")
-        w1_raw = sb.tile([P, PACK, R], F32, name="w1_raw", tag="w1_then_old")
+        words = sb.tile([P, T], U16, name="words", align_bytes=64)
+        scales = late.tile([P, T], U8, name="scales", align_bytes=64, offset=10496)
+        placed = late.tile([P, J], F32, name="placed", offset=0)
+        ones = late.tile([P, P], F32, name="ones", offset=1984)
+        gain_sb = late.tile([P, 1], F32, name="gain_sb", offset=2048)
+        share_sb = late.tile([P, 1], F32, name="share_sb", offset=2080)
+        dy_raw = late.tile([P, PACK, M], F32, name="dy_raw", offset=2112)
+        w1_raw = late.tile([P, PACK, R], F32, name="w1_raw", offset=6400)
+        wo_raw = sb.tile([P, PACK, R], F32, name="wo_raw")
         pb_cols = sb.tile([P, 2], F32, name="pb_cols")
         ident = sb.tile([P, P], F32, name="ident")
+        column = sb.tile([P, P], F32, name="column")
+        row = sb.tile([P, 1], F32, name="row")
 
         nc.vector.memset(scales[:].bitcast(I32), 0)
+        nc.vector.memset(ones[:], 1.0)
+        nc.vector.tensor_tensor_scan(column[:], ones[:], ones[:], -1.0, ALU.mult, ALU.add)
         nc.vector.memset(placed[:], 0.0)
-        share_sb = sb.tile([P, 1], F32, name="share_sb")
-        centre = sb.tile([P, 1], F32, name="centre")
-        nc.gpsimd.dma_start(share_sb[:], share)
+        nc.gpsimd.iota(row[:], [[0, 1]], base=0, channel_multiplier=1, allow_small_or_imprecise_dtypes=True)
         nc.gpsimd.dma_start(pb_cols[:], pb.rearrange("o (p e) -> p (o e)", e=2))
-        make_identity(nc, ident[:])
-        nc.gpsimd.tensor_scalar(centre[:], share_sb[:], -1.0 / RUN, 0.0, ALU.mult, ALU.add)
+        nc.gpsimd.dma_start(wo_raw[:], wo.rearrange("(p t) r -> p t r", t=PACK))
+        nc.vector.tensor_scalar(ident[:], column[:], row[:], None, ALU.is_equal)
         nc.sync.dma_start(idx[:], offs)
         nc.sync.dma_start(words[:].bitcast(I32), tab_words[0].bitcast(I32))
         nc.sync.dma_start(w1_raw[:], w1.rearrange("(p t) r -> p t r", t=PACK))
         nc.sync.dma_start(idx2[:], offs2)
-        nc.sync.dma_start(dy_raw[:], dy.rearrange("(p t) m -> p t m", t=PACK))
         for q in range(4):
-            nc.scalar.dma_start(
+            nc.sync.dma_start(
                 scales[32 * q : 32 * q + 4, :].bitcast(I32), tab_scales[0, 4 * q : 4 * q + 4, :].bitcast(I32)
             )
+        nc.sync.dma_start(dy_raw[:], dy.rearrange("(p t) m -> p t m", t=PACK))
+        nc.sync.dma_start(gain_sb[:], gain)
+        nc.sync.dma_start(share_sb[:], share)
 
-        def operand(name, width, pool=sb, offset=None):
-            grouped = pool.tile([P, width, PACK], BF16, name=name + "_bf", align_bytes=64, offset=offset)
-            codes = sb.tile([P, width], U32, name=name + "_codes", align_bytes=64)
-            plane = sb.tile([P, width], U8, name=name + "_plane", align_bytes=64)
-            return grouped, codes, plane
-
-        def quantise(op):
-            grouped, codes, plane = op
+        def quantise(grouped, codes, plane):
             nc.vector.quantize_mx(codes[:].bitcast(FP8X4), plane[:], grouped[:].rearrange("p c t -> p (c t)"))
 
-        w1_q = operand("w1", R)
-        dy_q = operand("dy", M, late, 5120)
+        w1_bf = sb.tile([P, R, PACK], BF16, name="w1_bf", align_bytes=64)
+        w1_codes = sb.tile([P, R], U32, name="w1_codes", align_bytes=64)
+        w1_plane = sb.tile([P, R], U8, name="w1_plane", align_bytes=64)
+        dy_codes = sb.tile([P, M], U32, name="dy_codes", align_bytes=64)
+        dy_plane = sb.tile([P, M], U8, name="dy_plane", align_bytes=64)
+        wo_plane = sb.tile([P, R], U8, name="wo_plane", align_bytes=64)
 
-        got_words = late.tile([P, J], U16, name="got_words", align_bytes=64, offset=4096)
+        got_words = late.tile([P, J], U16, name="got_words", align_bytes=64, offset=9472)
         got_scales = [sb.tile([P, JH], U8, name="got_scales%d" % h, align_bytes=64) for h in range(2)]
         a_ps = [ps.tile([P, JH], F32, name="a_ps%d" % h) for h in range(2)]
         c_ps = ps.tile([P, M], F32, name="c_ps")
         pb_ps = ps.tile([P, 2, P], F32, name="pb_ps")
         h0 = sb.tile([P, J], F32, name="h0")
         h0_sq = sb.tile([P, J], F32, name="h0_sq")
-        pb_rows = sb.tile([P, M], F32, name="pb_rows")
+        centre = sb.tile([P, 1], F32, name="centre")
 
-        dst, src = woven(w1_q[0][:], w1_raw[:])
+        dst, src = woven(w1_bf[:], w1_raw[:])
         nc.scalar.activation(dst, src, ACT.Copy)
-        nc.vector.tensor_copy(got_words[:], words[:].indirect(idx[:]))
-        gain_sb = late.tile([P, 1], F32, name="gain_sb", offset=0)
-        wo_raw = late.tile([P, PACK, R], F32, name="wo_raw", offset=128)
-        nc.sync.dma_start(gain_sb[:], gain)
-        nc.sync.dma_start(wo_raw[:], wo.rearrange("(p t) r -> p t r", t=PACK))
-        old_sb = sb.tile([P, J], F32, name="old_sb", tag="w1_then_old")
+        old_sb = late.tile([P, J], F32, name="old_sb", offset=7424)
         nc.sync.dma_start(old_sb[:], old)
-        quantise(w1_q)
+        nc.vector.tensor_copy(got_words[:], words[:].indirect(idx[:]))
+        quantise(w1_bf, w1_codes, w1_plane)
         for h in range(2):
             nc.vector.tensor_copy(got_scales[h][:], scales[:].indirect(idx[:, h * JH // LIST : (h + 1) * JH // LIST]))
+
+        pb_rows = late.tile([P, M], F32, name="pb_rows", offset=6400)
+        for e in range(2):
+            nc.tensor.transpose(pb_ps[:, e, :], pb_cols[:, e : e + 1].to_broadcast([P, P]), ident[:])
+        nc.scalar.copy(pb_rows[:].rearrange("r (p e) -> r p e", e=2), pb_ps[:].rearrange("r e p -> r p e"))
+        nc.gpsimd.tensor_scalar(centre[:], share_sb[:], -1.0 / RUN, 0.0, ALU.mult, ALU.add)
 
         for h in range(2):
             cols = slice(h * JH, (h + 1) * JH)
             nc.tensor.matmul_mx(
                 a_ps[h][:],
-                lhsT=w1_q[1][:].bitcast(FP8X4),
-                lhsT_scale=w1_q[2][:],
+                lhsT=w1_codes[:].bitcast(FP8X4),
+                lhsT_scale=w1_plane[:],
                 rhs=got_words[:, cols].bitcast(FP4X4),
                 rhs_scale=got_scales[h][:],
                 start=True,
@@ -117,30 +123,17 @@ def tile_attend_cpickcentred_kernel(tc, tab_words, tab_scales, w1, gain, share, 
             )
             nc.scalar.activation(h0[:, cols], a_ps[h][:], ACT.Tanh)
 
-        for e in range(2):
-            nc.tensor.transpose(pb_ps[:, e, :], pb_cols[:, e : e + 1].to_broadcast([P, P]), ident[:])
-        nc.scalar.copy(pb_rows[:].rearrange("r (p e) -> r p e", e=2), pb_ps[:].rearrange("r e p -> r p e"))
-
-        dst, src = woven(dy_q[0][:], dy_raw[:])
+        dy_bf = late.tile([P, M, PACK], BF16, name="dy_bf", align_bytes=64, offset=10496)
+        dst, src = woven(dy_bf[:], dy_raw[:])
         nc.vector.tensor_copy(dst, src)
-        quantise(dy_q)
-        h1 = late.tile([P, J], F32, name="h1", offset=5120)
+        quantise(dy_bf, dy_codes, dy_plane)
+        h1 = late.tile([P, J], F32, name="h1", offset=10496)
         for h in range(2):
             cols = slice(h * JH, (h + 1) * JH)
             nc.vector.tensor_scalar(h1[:, cols], h0[:, cols], gain_sb[:], None, ALU.mult)
-        wo_q = operand("wo", R, late, 4096)
-        dst, src = woven(wo_q[0][:], wo_raw[:])
+        wo_bf = late.tile([P, R, PACK], BF16, name="wo_bf", align_bytes=64, offset=9472)
+        dst, src = woven(wo_bf[:], wo_raw[:])
         nc.scalar.activation(dst, src, ACT.Copy)
-        quantise(wo_q)
-        nc.tensor.matmul_mx(
-            c_ps[:],
-            lhsT=wo_q[1][:].bitcast(FP8X4),
-            lhsT_scale=wo_q[2][:],
-            rhs=dy_q[1][:].bitcast(FP8X4),
-            rhs_scale=dy_q[2][:],
-            start=True,
-            stop=True,
-        )
 
         def halves(name, width):
             return [sb.tile([P, width], F32, name="%s%d" % (name, h)) for h in range(2)]
@@ -159,6 +152,17 @@ def tile_attend_cpickcentred_kernel(tc, tab_words, tab_scales, w1, gain, share, 
             nc.vector.tensor_tensor(s[h][:], h1[:].indirect(picks[h]), pb_rows[:, h * MH : (h + 1) * MH], ALU.add)
         for h in range(2):
             nc.vector.tensor_reduce(s_sum[h][:], runs(s[h]), mybir.AxisListType.X, ALU.add)
+        wo_codes = late.tile([P, R], U32, name="wo_codes", align_bytes=64, offset=10496)
+        quantise(wo_bf, wo_codes, wo_plane)
+        nc.tensor.matmul_mx(
+            c_ps[:],
+            lhsT=wo_codes[:].bitcast(FP8X4),
+            lhsT_scale=wo_plane[:],
+            rhs=dy_codes[:].bitcast(FP8X4),
+            rhs_scale=dy_plane[:],
+            start=True,
+            stop=True,
+        )
         for h in range(2):
             nc.vector.scalar_tensor_tensor(runs(z[h]), spread(s_sum[h]), centre[:], runs(s[h]), ALU.mult, ALU.add)
             nc.scalar.activation(th[h][:], z[h][:], ACT.Tanh, scale=-0.5)

@@ -1,4 +1,3 @@
-import math
 from contextlib import ExitStack
 
 import concourse.mybir as mybir
@@ -21,126 +20,44 @@ P = 128
 PACK = 4
 RUN = M // G
 LIST = 16
+QUADRANT = 32
+NEIGHBOURS = 4
+JH, MH, GH = J // 2, M // 2, G // 2
+FINITE = 3.0e38
+
+AT_WO = 0
+AT_DY = AT_WO + 4 * PACK * R
+AT_ONES = AT_DY - 64
+AT_W1 = AT_DY + 4 * PACK * M
+AT_OLD = AT_W1 + 2 * PACK * R
+AT_GOT = AT_OLD + 4 * J
+AT_SCALES = AT_GOT + 2 * J
+AT_H1 = AT_SCALES + 64
 
 
 def woven(grouped, raw):
     return (
-        grouped.rearrange("p (c i) t -> p c t i", i=4),
-        raw.rearrange("p t (c i) -> p c t i", i=4),
+        grouped.rearrange("p (c i) t -> p c t i", i=NEIGHBOURS),
+        raw.rearrange("p t (c i) -> p c t i", i=NEIGHBOURS),
     )
+
+
+def half(h, width):
+    return slice(h * width, (h + 1) * width)
 
 
 def tile_attend_cpickcentred_kernel(tc, tab_words, tab_scales, w1, gain, share, pb, wo, dy, old, offs, offs2, out):
     nc = tc.nc
-    JH = J // 2
-    MH = M // 2
-    GH = G // 2
     with ExitStack() as ctx:
         sb = ctx.enter_context(tc.tile_pool(name="sb", bufs=1))
-        late = ctx.enter_context(tc.tile_pool(name="late", bufs=1))
+        shared = ctx.enter_context(tc.tile_pool(name="shared", bufs=1))
         ps = ctx.enter_context(tc.psum_pool(name="ps", bufs=1))
 
-        idx = sb.tile([P, J // LIST], U16, name="idx")
-        idx2 = sb.tile([P, M // LIST], U16, name="idx2")
-        words = sb.tile([P, T], U16, name="words", align_bytes=64)
-        scales = late.tile([P, T], U8, name="scales", align_bytes=64, offset=10496)
-        placed = late.tile([P, J], F32, name="placed", offset=0)
-        ones = late.tile([P, P], F32, name="ones", offset=1984)
-        gain_sb = late.tile([P, 1], F32, name="gain_sb", offset=2048)
-        share_sb = late.tile([P, 1], F32, name="share_sb", offset=2080)
-        dy_raw = late.tile([P, PACK, M], F32, name="dy_raw", offset=2112)
-        w1_raw = late.tile([P, PACK, R], F32, name="w1_raw", offset=6400)
-        wo_raw = sb.tile([P, PACK, R], F32, name="wo_raw")
-        pb_cols = sb.tile([P, 2], F32, name="pb_cols")
-        ident = sb.tile([P, P], F32, name="ident")
-        column = sb.tile([P, P], F32, name="column")
-        row = sb.tile([P, 1], F32, name="row")
-
-        nc.vector.memset(scales[:].bitcast(I32), 0)
-        nc.vector.memset(ones[:], 1.0)
-        nc.vector.tensor_tensor_scan(column[:], ones[:], ones[:], -1.0, ALU.mult, ALU.add)
-        nc.vector.memset(placed[:], 0.0)
-        nc.gpsimd.iota(row[:], [[0, 1]], base=0, channel_multiplier=1, allow_small_or_imprecise_dtypes=True)
-        nc.gpsimd.dma_start(pb_cols[:], pb.rearrange("o (p e) -> p (o e)", e=2))
-        nc.gpsimd.dma_start(wo_raw[:], wo.rearrange("(p t) r -> p t r", t=PACK))
-        nc.vector.tensor_scalar(ident[:], column[:], row[:], None, ALU.is_equal)
-        nc.sync.dma_start(idx[:], offs)
-        nc.sync.dma_start(words[:].bitcast(I32), tab_words[0].bitcast(I32))
-        nc.sync.dma_start(w1_raw[:], w1.rearrange("(p t) r -> p t r", t=PACK))
-        nc.sync.dma_start(idx2[:], offs2)
-        for q in range(4):
-            nc.sync.dma_start(
-                scales[32 * q : 32 * q + 4, :].bitcast(I32), tab_scales[0, 4 * q : 4 * q + 4, :].bitcast(I32)
-            )
-        nc.sync.dma_start(dy_raw[:], dy.rearrange("(p t) m -> p t m", t=PACK))
-        nc.sync.dma_start(gain_sb[:], gain)
-        nc.sync.dma_start(share_sb[:], share)
-
         def quantise(grouped, codes, plane):
-            nc.vector.quantize_mx(codes[:].bitcast(FP8X4), plane[:], grouped[:].rearrange("p c t -> p (c t)"))
-
-        w1_bf = sb.tile([P, R, PACK], BF16, name="w1_bf", align_bytes=64)
-        w1_codes = sb.tile([P, R], U32, name="w1_codes", align_bytes=64)
-        w1_plane = sb.tile([P, R], U8, name="w1_plane", align_bytes=64)
-        dy_codes = sb.tile([P, M], U32, name="dy_codes", align_bytes=64)
-        dy_plane = sb.tile([P, M], U8, name="dy_plane", align_bytes=64)
-        wo_plane = sb.tile([P, R], U8, name="wo_plane", align_bytes=64)
-
-        got_words = late.tile([P, J], U16, name="got_words", align_bytes=64, offset=9472)
-        got_scales = [sb.tile([P, JH], U8, name="got_scales%d" % h, align_bytes=64) for h in range(2)]
-        a_ps = [ps.tile([P, JH], F32, name="a_ps%d" % h) for h in range(2)]
-        c_ps = ps.tile([P, M], F32, name="c_ps")
-        pb_ps = ps.tile([P, 2, P], F32, name="pb_ps")
-        h0 = sb.tile([P, J], F32, name="h0")
-        h0_sq = sb.tile([P, J], F32, name="h0_sq")
-        centre = sb.tile([P, 1], F32, name="centre")
-
-        dst, src = woven(w1_bf[:], w1_raw[:])
-        nc.scalar.activation(dst, src, ACT.Copy)
-        old_sb = late.tile([P, J], F32, name="old_sb", offset=7424)
-        nc.sync.dma_start(old_sb[:], old)
-        nc.vector.tensor_copy(got_words[:], words[:].indirect(idx[:]))
-        quantise(w1_bf, w1_codes, w1_plane)
-        for h in range(2):
-            nc.vector.tensor_copy(got_scales[h][:], scales[:].indirect(idx[:, h * JH // LIST : (h + 1) * JH // LIST]))
-
-        pb_rows = late.tile([P, M], F32, name="pb_rows", offset=6400)
-        for e in range(2):
-            nc.tensor.transpose(pb_ps[:, e, :], pb_cols[:, e : e + 1].to_broadcast([P, P]), ident[:])
-        nc.scalar.copy(pb_rows[:].rearrange("r (p e) -> r p e", e=2), pb_ps[:].rearrange("r e p -> r p e"))
-        nc.gpsimd.tensor_scalar(centre[:], share_sb[:], -1.0 / RUN, 0.0, ALU.mult, ALU.add)
-
-        for h in range(2):
-            cols = slice(h * JH, (h + 1) * JH)
-            nc.tensor.matmul_mx(
-                a_ps[h][:],
-                lhsT=w1_codes[:].bitcast(FP8X4),
-                lhsT_scale=w1_plane[:],
-                rhs=got_words[:, cols].bitcast(FP4X4),
-                rhs_scale=got_scales[h][:],
-                start=True,
-                stop=True,
-            )
-            nc.scalar.activation(h0[:, cols], a_ps[h][:], ACT.Tanh)
-
-        dy_bf = late.tile([P, M, PACK], BF16, name="dy_bf", align_bytes=64, offset=10496)
-        dst, src = woven(dy_bf[:], dy_raw[:])
-        nc.vector.tensor_copy(dst, src)
-        quantise(dy_bf, dy_codes, dy_plane)
-        h1 = late.tile([P, J], F32, name="h1", offset=10496)
-        for h in range(2):
-            cols = slice(h * JH, (h + 1) * JH)
-            nc.vector.tensor_scalar(h1[:, cols], h0[:, cols], gain_sb[:], None, ALU.mult)
-        wo_bf = late.tile([P, R, PACK], BF16, name="wo_bf", align_bytes=64, offset=9472)
-        dst, src = woven(wo_bf[:], wo_raw[:])
-        nc.scalar.activation(dst, src, ACT.Copy)
+            nc.vector.quantize_mx(codes.bitcast(FP8X4), plane, grouped.rearrange("p c t -> p (c t)"))
 
         def halves(name, width):
             return [sb.tile([P, width], F32, name="%s%d" % (name, h)) for h in range(2)]
-
-        s, z, th, g2, r2 = (halves(n, MH) for n in ("s", "z", "th", "g2", "r2"))
-        s_sum, g_sum = halves("s_sum", GH), halves("g_sum", GH)
-        picks = [idx2[:, h * MH // LIST : (h + 1) * MH // LIST] for h in range(2)]
 
         def runs(tile):
             return tile[:].rearrange("r (g e) -> r g e", e=RUN)
@@ -148,12 +65,110 @@ def tile_attend_cpickcentred_kernel(tc, tab_words, tab_scales, w1, gain, share, 
         def spread(tile):
             return tile[:].unsqueeze(2).to_broadcast([P, GH, RUN])
 
+        idx = sb.tile([P, J // LIST], U16, name="idx")
+        idx2 = sb.tile([P, M // LIST], U16, name="idx2")
+        words = sb.tile([P, T], U16, name="words", align_bytes=64)
+        scales = shared.tile([P, T], U8, name="scales", align_bytes=64, offset=AT_SCALES)
+        placed = sb.tile([P, J], F32, name="placed")
+        ones = shared.tile([P, P], F32, name="ones", offset=AT_ONES)
+        gain_sb = sb.tile([P, 1], F32, name="gain_sb")
+        share_sb = sb.tile([P, 1], F32, name="share_sb")
+        wo_raw = shared.tile([P, PACK, R], F32, name="wo_raw", offset=AT_WO)
+        dy_raw = shared.tile([P, PACK, M], F32, name="dy_raw", offset=AT_DY)
+        w1_raw = shared.tile([P, PACK, R], F32, name="w1_raw", offset=AT_W1)
+        pb_cols = sb.tile([P, 2], F32, name="pb_cols")
+        ident = sb.tile([P, P], F32, name="ident")
+        column = sb.tile([P, P], F32, name="column")
+        row = sb.tile([P, 1], F32, name="row")
+
+        nc.vector.memset(ones[:], 1.0)
+        nc.vector.memset(scales[:].bitcast(I32), 0)
+        nc.vector.tensor_tensor_scan(column[:], ones[:], ones[:], -1.0, ALU.mult, ALU.add)
+        nc.vector.memset(placed[:], 0.0)
+        nc.gpsimd.iota(row[:], [[0, 1]], base=0, channel_multiplier=1, allow_small_or_imprecise_dtypes=True)
+        nc.gpsimd.dma_start(gain_sb[:], gain)
+        nc.gpsimd.dma_start(pb_cols[:], pb.rearrange("o (p e) -> p (o e)", e=2))
+        nc.gpsimd.dma_start(share_sb[:], share)
+        nc.vector.tensor_scalar(ident[:], column[:], row[:], None, ALU.is_equal)
+
+        nc.sync.dma_start(idx[:], offs)
+        nc.sync.dma_start(words[:].bitcast(I32), tab_words[0].bitcast(I32))
+        nc.sync.dma_start(w1_raw[:], w1.rearrange("(p t) r -> p t r", t=PACK))
+        nc.sync.dma_start(idx2[:], offs2)
+        for q in range(P // QUADRANT):
+            nc.sync.dma_start(
+                scales[QUADRANT * q : QUADRANT * q + 4, :].bitcast(I32),
+                tab_scales[0, 4 * q : 4 * q + 4, :].bitcast(I32),
+            )
+        nc.sync.dma_start(dy_raw[:], dy.rearrange("(p t) m -> p t m", t=PACK))
+        nc.sync.dma_start(wo_raw[:], wo.rearrange("(p t) r -> p t r", t=PACK))
+
+        w1_bf = sb.tile([P, R, PACK], BF16, name="w1_bf", align_bytes=64)
+        w1_codes = sb.tile([P, R], U32, name="w1_codes", align_bytes=64)
+        w1_plane = sb.tile([P, R], U8, name="w1_plane", align_bytes=64)
+        dy_codes = sb.tile([P, M], U32, name="dy_codes", align_bytes=64)
+        dy_plane = sb.tile([P, M], U8, name="dy_plane", align_bytes=64)
+        wo_plane = sb.tile([P, R], U8, name="wo_plane", align_bytes=64)
+        got_words = shared.tile([P, J], U16, name="got_words", align_bytes=64, offset=AT_GOT)
+        got_scales = [sb.tile([P, JH], U8, name="got_scales%d" % h, align_bytes=64) for h in range(2)]
+        a_ps = [ps.tile([P, JH], F32, name="a_ps%d" % h) for h in range(2)]
+        c_ps = ps.tile([P, M], F32, name="c_ps")
+        pb_ps = ps.tile([P, 2, P], F32, name="pb_ps")
+        centre = sb.tile([P, 1], F32, name="centre")
+
+        dst, src = woven(w1_bf[:], w1_raw[:])
+        nc.scalar.activation(dst, src, ACT.Copy)
+        old_sb = shared.tile([P, J], F32, name="old_sb", offset=AT_OLD)
+        nc.sync.dma_start(old_sb[:], old)
+        nc.vector.tensor_copy(got_words[:], words[:].indirect(idx[:]))
+        quantise(w1_bf[:], w1_codes[:], w1_plane[:])
         for h in range(2):
-            nc.vector.tensor_tensor(s[h][:], h1[:].indirect(picks[h]), pb_rows[:, h * MH : (h + 1) * MH], ALU.add)
+            nc.vector.tensor_copy(got_scales[h][:], scales[:].indirect(idx[:, half(h, JH // LIST)]))
+
+        for e in range(2):
+            nc.tensor.transpose(pb_ps[:, e, :], pb_cols[:, e : e + 1].to_broadcast([P, P]), ident[:])
+        nc.gpsimd.tensor_scalar(centre[:], share_sb[:], -1.0 / RUN, 0.0, ALU.mult, ALU.add)
+
+        h0 = sb.tile([P, J], F32, name="h0")
         for h in range(2):
-            nc.vector.tensor_reduce(s_sum[h][:], runs(s[h]), mybir.AxisListType.X, ALU.add)
-        wo_codes = late.tile([P, R], U32, name="wo_codes", align_bytes=64, offset=10496)
-        quantise(wo_bf, wo_codes, wo_plane)
+            nc.tensor.matmul_mx(
+                a_ps[h][:],
+                lhsT=w1_codes[:].bitcast(FP8X4),
+                lhsT_scale=w1_plane[:],
+                rhs=got_words[:, half(h, JH)].bitcast(FP4X4),
+                rhs_scale=got_scales[h][:],
+                start=True,
+                stop=True,
+            )
+            nc.scalar.activation(h0[:, half(h, JH)], a_ps[h][:], ACT.Tanh)
+
+        dy_bf = shared.tile([P, M, PACK], BF16, name="dy_bf", align_bytes=64, offset=AT_H1)
+        inv_raw = shared.tile([P, 1], F32, name="inv_raw", offset=AT_SCALES)
+        inv_gain = sb.tile([P, 1], F32, name="inv_gain")
+        dst, src = woven(dy_bf[:], dy_raw[:])
+        nc.vector.tensor_copy(dst, src)
+        nc.vector.reciprocal(inv_raw[:], gain_sb[:])
+        quantise(dy_bf[:], dy_codes[:], dy_plane[:])
+        nc.vector.tensor_scalar(inv_gain[:], inv_raw[:], FINITE, -FINITE, ALU.min, ALU.max)
+        h1 = shared.tile([P, J], F32, name="h1", offset=AT_H1)
+        for h in range(2):
+            nc.vector.tensor_scalar(h1[:, half(h, JH)], h0[:, half(h, JH)], gain_sb[:], None, ALU.mult)
+
+        wo_bf = shared.tile([P, R, PACK], BF16, name="wo_bf", align_bytes=64, offset=AT_GOT)
+        dst, src = woven(wo_bf[:], wo_raw[:])
+        nc.scalar.activation(dst, src, ACT.Copy)
+
+        s, z, th, g2, ds2 = (halves(name, MH) for name in ("s", "z", "th", "g2", "ds2"))
+        s_sum, g_sum = halves("s_sum", GH), halves("g_sum", GH)
+        picked = sb.tile([P, M], F32, name="picked")
+        h0_sq = shared.tile([P, M], F32, name="h0_sq", offset=AT_WO)
+        slope = sb.tile([P, M], F32, name="slope")
+        picks = [idx2[:, half(h, MH // LIST)] for h in range(2)]
+
+        for h in range(2):
+            nc.vector.tensor_copy(picked[:, half(h, MH)], h1[:].indirect(picks[h]))
+        wo_codes = shared.tile([P, R], U32, name="wo_codes", align_bytes=64, offset=AT_H1)
+        quantise(wo_bf[:], wo_codes[:], wo_plane[:])
         nc.tensor.matmul_mx(
             c_ps[:],
             lhsT=wo_codes[:].bitcast(FP8X4),
@@ -163,24 +178,33 @@ def tile_attend_cpickcentred_kernel(tc, tab_words, tab_scales, w1, gain, share, 
             start=True,
             stop=True,
         )
+
+        nc.scalar.activation(h0_sq[:], picked[:], ACT.Square, scale=inv_gain[:])
+        for h in range(2):
+            nc.vector.tensor_tensor(
+                s[h][:].rearrange("r (p e) -> r p e", e=2),
+                picked[:, half(h, MH)].rearrange("r (p e) -> r p e", e=2),
+                pb_ps[:, :, half(h, MH // 2)].rearrange("r e p -> r p e"),
+                ALU.add,
+            )
+        for h in range(2):
+            nc.vector.tensor_reduce(s_sum[h][:], runs(s[h]), mybir.AxisListType.X, ALU.add)
+
         for h in range(2):
             nc.vector.scalar_tensor_tensor(runs(z[h]), spread(s_sum[h]), centre[:], runs(s[h]), ALU.mult, ALU.add)
             nc.scalar.activation(th[h][:], z[h][:], ACT.Tanh, scale=-0.5)
-        nc.scalar.activation(h0_sq[:], h0[:], ACT.Square, scale=math.sqrt(0.5))
+        nc.scalar.activation(slope[:], h0_sq[:], ACT.Copy, scale=0.5, bias=-0.5)
         for h in range(2):
-            nc.vector.scalar_tensor_tensor(g2[h][:], th[h][:], 1.0, c_ps[:, h * MH : (h + 1) * MH], ALU.subtract, ALU.mult)
+            nc.vector.scalar_tensor_tensor(g2[h][:], th[h][:], 1.0, c_ps[:, half(h, MH)], ALU.subtract, ALU.mult)
         for h in range(2):
             nc.vector.tensor_reduce(g_sum[h][:], runs(g2[h]), mybir.AxisListType.X, ALU.add)
         for h in range(2):
-            nc.vector.tensor_scalar(runs(r2[h]), spread(g_sum[h]), centre[:], None, ALU.mult)
-        for h in range(2):
-            nc.vector.tensor_tensor(placed[:].indirect(picks[h]), g2[h][:], r2[h][:], ALU.add)
+            nc.vector.scalar_tensor_tensor(runs(ds2[h]), spread(g_sum[h]), centre[:], runs(g2[h]), ALU.mult, ALU.add)
 
-        da, res = halves("da", JH), halves("res", JH)
         for h in range(2):
-            cols = slice(h * JH, (h + 1) * JH)
-            nc.vector.scalar_tensor_tensor(da[h][:], h0_sq[:, cols], 0.5, placed[:, cols], ALU.subtract, ALU.mult)
+            nc.vector.tensor_tensor(placed[:].indirect(picks[h]), ds2[h][:], slope[:, half(h, MH)], ALU.mult)
+        res = halves("res", JH)
         for h, queue in enumerate((nc.sync, nc.scalar)):
-            cols = slice(h * JH, (h + 1) * JH)
-            nc.vector.scalar_tensor_tensor(res[h][:], da[h][:], gain_sb[:], old_sb[:, cols], ALU.mult, ALU.add)
+            cols = half(h, JH)
+            nc.vector.scalar_tensor_tensor(res[h][:], placed[:, cols], gain_sb[:], old_sb[:, cols], ALU.mult, ALU.add)
             queue.dma_start(out[:, cols], res[h][:])

from contextlib import ExitStack

import concourse.mybir as mybir

K, R, F, T, J, M, G = 512, 128, 512, 2048, 512, 256, 32
FLOPS = 2 * K * R * J + 2 * F * R * M

F32 = mybir.dt.float32
BF16 = mybir.dt.bfloat16
I32 = mybir.dt.int32
U32 = mybir.dt.uint32
U16 = mybir.dt.uint16
U8 = mybir.dt.uint8
FP8X4 = mybir.dt.float8_e4m3fn_x4
FP4X4 = mybir.dt.float4_e2m1fn_x4
ALU = mybir.AluOpType
ACT = mybir.ActivationFunctionType

P = 128
PACK = 4
RUN = M // G
LIST = 16
QUADRANT = 32
NEIGHBOURS = 4
JH, MH, GH = J // 2, M // 2, G // 2
FINITE = 3.0e38

AT_WO = 0
AT_DY = AT_WO + 4 * PACK * R
AT_ONES = AT_DY - 64
AT_W1 = AT_DY + 4 * PACK * M
AT_OLD = AT_W1 + 2 * PACK * R
AT_GOT = AT_OLD + 4 * J
AT_SCALES = AT_GOT + 2 * J
AT_H1 = AT_SCALES + 64


def woven(grouped, raw):
    return (
        grouped.rearrange("p (c i) t -> p c t i", i=NEIGHBOURS),
        raw.rearrange("p t (c i) -> p c t i", i=NEIGHBOURS),
    )


def half(h, width):
    return slice(h * width, (h + 1) * width)


def tile_attend_cpickcentred_kernel(tc, tab_words, tab_scales, w1, gain, share, pb, wo, dy, old, offs, offs2, out):
    nc = tc.nc
    with ExitStack() as ctx:
        sb = ctx.enter_context(tc.tile_pool(name="sb", bufs=1))
        shared = ctx.enter_context(tc.tile_pool(name="shared", bufs=1))
        ps = ctx.enter_context(tc.psum_pool(name="ps", bufs=1))

        def quantise(grouped, codes, plane):
            nc.vector.quantize_mx(codes.bitcast(FP8X4), plane, grouped.rearrange("p c t -> p (c t)"))

        def halves(name, width):
            return [sb.tile([P, width], F32, name="%s%d" % (name, h)) for h in range(2)]

        def runs(tile):
            return tile[:].rearrange("r (g e) -> r g e", e=RUN)

        def spread(tile):
            return tile[:].unsqueeze(2).to_broadcast([P, GH, RUN])

        idx = sb.tile([P, J // LIST], U16, name="idx")
        idx2 = sb.tile([P, M // LIST], U16, name="idx2")
        words = sb.tile([P, T], U16, name="words", align_bytes=64)
        scales = shared.tile([P, T], U8, name="scales", align_bytes=64, offset=AT_SCALES)
        placed = sb.tile([P, J], F32, name="placed")
        ones = shared.tile([P, P], F32, name="ones", offset=AT_ONES)
        gain_sb = sb.tile([P, 1], F32, name="gain_sb")
        share_sb = sb.tile([P, 1], F32, name="share_sb")
        wo_raw = shared.tile([P, PACK, R], F32, name="wo_raw", offset=AT_WO)
        dy_raw = shared.tile([P, PACK, M], F32, name="dy_raw", offset=AT_DY)
        w1_raw = shared.tile([P, PACK, R], F32, name="w1_raw", offset=AT_W1)
        pb_cols = sb.tile([P, 2], F32, name="pb_cols")
        ident = sb.tile([P, P], F32, name="ident")
        column = sb.tile([P, P], F32, name="column")
        row = sb.tile([P, 1], F32, name="row")

        nc.vector.memset(ones[:], 1.0)
        nc.vector.memset(scales[:].bitcast(I32), 0)
        nc.vector.tensor_tensor_scan(column[:], ones[:], ones[:], -1.0, ALU.mult, ALU.add)
        nc.vector.memset(placed[:], 0.0)
        nc.gpsimd.iota(row[:], [[0, 1]], base=0, channel_multiplier=1, allow_small_or_imprecise_dtypes=True)
        nc.gpsimd.dma_start(gain_sb[:], gain)
        nc.gpsimd.dma_start(pb_cols[:], pb.rearrange("o (p e) -> p (o e)", e=2))
        nc.gpsimd.dma_start(share_sb[:], share)
        nc.vector.tensor_scalar(ident[:], column[:], row[:], None, ALU.is_equal)

        nc.sync.dma_start(idx[:], offs)
        nc.sync.dma_start(words[:].bitcast(I32), tab_words[0].bitcast(I32))
        nc.sync.dma_start(w1_raw[:], w1.rearrange("(p t) r -> p t r", t=PACK))
        nc.sync.dma_start(idx2[:], offs2)
        for q in range(P // QUADRANT):
            nc.sync.dma_start(
                scales[QUADRANT * q : QUADRANT * q + 4, :].bitcast(I32),
                tab_scales[0, 4 * q : 4 * q + 4, :].bitcast(I32),
            )
        nc.sync.dma_start(dy_raw[:], dy.rearrange("(p t) m -> p t m", t=PACK))
        nc.sync.dma_start(wo_raw[:], wo.rearrange("(p t) r -> p t r", t=PACK))

        w1_bf = sb.tile([P, R, PACK], BF16, name="w1_bf", align_bytes=64)
        w1_codes = sb.tile([P, R], U32, name="w1_codes", align_bytes=64)
        w1_plane = sb.tile([P, R], U8, name="w1_plane", align_bytes=64)
        dy_codes = sb.tile([P, M], U32, name="dy_codes", align_bytes=64)
        dy_plane = sb.tile([P, M], U8, name="dy_plane", align_bytes=64)
        wo_plane = sb.tile([P, R], U8, name="wo_plane", align_bytes=64)
        got_words = shared.tile([P, J], U16, name="got_words", align_bytes=64, offset=AT_GOT)
        got_scales = [sb.tile([P, JH], U8, name="got_scales%d" % h, align_bytes=64) for h in range(2)]
        a_ps = [ps.tile([P, JH], F32, name="a_ps%d" % h) for h in range(2)]
        c_ps = ps.tile([P, M], F32, name="c_ps")
        pb_ps = ps.tile([P, 2, P], F32, name="pb_ps")
        centre = sb.tile([P, 1], F32, name="centre")

        dst, src = woven(w1_bf[:], w1_raw[:])
        nc.scalar.activation(dst, src, ACT.Copy)
        old_sb = shared.tile([P, J], F32, name="old_sb", offset=AT_OLD)
        nc.sync.dma_start(old_sb[:], old)
        nc.vector.tensor_copy(got_words[:], words[:].indirect(idx[:]))
        quantise(w1_bf[:], w1_codes[:], w1_plane[:])
        for h in range(2):
            nc.vector.tensor_copy(got_scales[h][:], scales[:].indirect(idx[:, half(h, JH // LIST)]))

        for e in range(2):
            nc.tensor.transpose(pb_ps[:, e, :], pb_cols[:, e : e + 1].to_broadcast([P, P]), ident[:])
        nc.gpsimd.tensor_scalar(centre[:], share_sb[:], -1.0 / RUN, 0.0, ALU.mult, ALU.add)

        h0 = sb.tile([P, J], F32, name="h0")
        for h in range(2):
            nc.tensor.matmul_mx(
                a_ps[h][:],
                lhsT=w1_codes[:].bitcast(FP8X4),
                lhsT_scale=w1_plane[:],
                rhs=got_words[:, half(h, JH)].bitcast(FP4X4),
                rhs_scale=got_scales[h][:],
                start=True,
                stop=True,
            )
            nc.scalar.activation(h0[:, half(h, JH)], a_ps[h][:], ACT.Tanh)

        dy_bf = shared.tile([P, M, PACK], BF16, name="dy_bf", align_bytes=64, offset=AT_H1)
        inv_raw = shared.tile([P, 1], F32, name="inv_raw", offset=AT_SCALES)
        inv_gain = sb.tile([P, 1], F32, name="inv_gain")
        dst, src = woven(dy_bf[:], dy_raw[:])
        nc.vector.tensor_copy(dst, src)
        nc.vector.reciprocal(inv_raw[:], gain_sb[:])
        quantise(dy_bf[:], dy_codes[:], dy_plane[:])
        nc.vector.tensor_scalar(inv_gain[:], inv_raw[:], FINITE, -FINITE, ALU.min, ALU.max)
        h1 = shared.tile([P, J], F32, name="h1", offset=AT_H1)
        for h in range(2):
            nc.vector.tensor_scalar(h1[:, half(h, JH)], h0[:, half(h, JH)], gain_sb[:], None, ALU.mult)

        wo_bf = shared.tile([P, R, PACK], BF16, name="wo_bf", align_bytes=64, offset=AT_GOT)
        dst, src = woven(wo_bf[:], wo_raw[:])
        nc.scalar.activation(dst, src, ACT.Copy)

        s, z, th, g2, ds2 = (halves(name, MH) for name in ("s", "z", "th", "g2", "ds2"))
        s_sum, g_sum = halves("s_sum", GH), halves("g_sum", GH)
        picked = sb.tile([P, M], F32, name="picked")
        h0_sq = shared.tile([P, M], F32, name="h0_sq", offset=AT_WO)
        slope = sb.tile([P, M], F32, name="slope")
        picks = [idx2[:, half(h, MH // LIST)] for h in range(2)]

        for h in range(2):
            nc.vector.tensor_copy(picked[:, half(h, MH)], h1[:].indirect(picks[h]))
        wo_codes = shared.tile([P, R], U32, name="wo_codes", align_bytes=64, offset=AT_H1)
        quantise(wo_bf[:], wo_codes[:], wo_plane[:])
        nc.tensor.matmul_mx(
            c_ps[:],
            lhsT=wo_codes[:].bitcast(FP8X4),
            lhsT_scale=wo_plane[:],
            rhs=dy_codes[:].bitcast(FP8X4),
            rhs_scale=dy_plane[:],
            start=True,
            stop=True,
        )

        nc.scalar.activation(h0_sq[:], picked[:], ACT.Square, scale=inv_gain[:])
        for h in range(2):
            nc.vector.tensor_tensor(
                s[h][:].rearrange("r (p e) -> r p e", e=2),
                picked[:, half(h, MH)].rearrange("r (p e) -> r p e", e=2),
                pb_ps[:, :, half(h, MH // 2)].rearrange("r e p -> r p e"),
                ALU.add,
            )
        for h in range(2):
            nc.vector.tensor_reduce(s_sum[h][:], runs(s[h]), mybir.AxisListType.X, ALU.add)

        for h in range(2):
            nc.vector.scalar_tensor_tensor(runs(z[h]), spread(s_sum[h]), centre[:], runs(s[h]), ALU.mult, ALU.add)
            nc.scalar.activation(th[h][:], z[h][:], ACT.Tanh, scale=-0.5)
        nc.scalar.activation(slope[:], h0_sq[:], ACT.Copy, scale=0.5, bias=-0.5)
        for h in range(2):
            nc.vector.scalar_tensor_tensor(g2[h][:], th[h][:], 1.0, c_ps[:, half(h, MH)], ALU.subtract, ALU.mult)
        for h in range(2):
            nc.vector.tensor_reduce(g_sum[h][:], runs(g2[h]), mybir.AxisListType.X, ALU.add)
        for h in range(2):
            nc.vector.scalar_tensor_tensor(runs(ds2[h]), spread(g_sum[h]), centre[:], runs(g2[h]), ALU.mult, ALU.add)

        for h in range(2):
            nc.vector.tensor_tensor(placed[:].indirect(picks[h]), ds2[h][:], slope[:, half(h, MH)], ALU.mult)
        res = halves("res", JH)
        for h, queue in enumerate((nc.sync, nc.scalar)):
            cols = half(h, JH)
            nc.vector.scalar_tensor_tensor(res[h][:], placed[:, cols], gain_sb[:], old_sb[:, cols], ALU.mult, ALU.add)
            queue.dma_start(out[:, cols], res[h][:])
